import numpy as np
import ml_dtypes


def mxq(x, axis, fmt="e4m3"):
    dtype, down = {"e4m3": (ml_dtypes.float8_e4m3fn, 7), "e5m2": (ml_dtypes.float8_e5m2, 14)}[fmt]
    v = np.moveaxis(np.asarray(x, np.float32).astype(ml_dtypes.bfloat16).astype(np.float64), axis, -1)
    blocks = v.reshape(v.shape[:-1] + (-1, 32))
    amax = np.abs(blocks).max(-1, keepdims=True)
    byte = np.maximum(np.where(amax > 0, np.frexp(amax)[1] - 1 + 127, 0) - down, 1)
    scale = np.exp2(byte - 127.0)
    codes = (blocks / scale).astype(np.float32).astype(dtype).astype(np.float64)
    return np.moveaxis((codes * scale).reshape(v.shape), -1, axis)


WIDE = False


def mx_kscale(k):
    if not WIDE:
        return np.ones(k)
    levels = np.array([10, -10, 5, -5, 0])
    if k % 512:
        return np.exp2(np.random.permutation(np.resize(levels, k // 32))).repeat(32)
    a = np.empty((k // 512, 16))
    for p in range(k // 512):
        a[p, :8] = np.random.permutation(np.resize(levels, 8))
        for g in range(8):
            far = levels[np.abs(levels - a[p, g]) >= 10]
            a[p, g + 8] = far[np.random.randint(len(far))]
    return np.exp2(a.ravel()).repeat(32)


BF16 = ml_dtypes.bfloat16


def bf(x):
    return np.asarray(x, np.float32).astype(BF16)


def f64(x):
    return np.asarray(x).astype(np.float64)


E2M1 = np.array([0.0, 0.5, 1.0, 1.5, 2.0, 3.0, 4.0, 6.0, -0.0, -0.5, -1.0, -1.5, -2.0, -3.0, -4.0, -6.0])


def pack_weight(w, fmt):
    k, n = w.shape
    w = f64(bf(w)).reshape(k // 32, 32, n)
    amax = np.abs(w).max(1)
    if fmt == "e4m3":
        byte = np.frexp(amax)[1] - 1 + 127 - 7
    else:
        mant, ex = np.frexp(amax / 6.0)
        byte = np.where(mant > 0.5, ex, ex - 1) + 127
    byte = np.clip(np.where(amax > 0, byte, 1), 1, 254)
    scaled = (w * np.exp2(127.0 - byte)[:, None, :]).reshape(k, n).astype(np.float32)
    by_word = np.ascontiguousarray(scaled.reshape(k // 512, 128, 4, n).transpose(0, 1, 3, 2))
    if fmt == "e4m3":
        words = by_word.astype(ml_dtypes.float8_e4m3fn).view(np.uint8)
    else:
        c = by_word.astype(ml_dtypes.float4_e2m1fn).view(np.uint8) & 0xF
        words = c[..., 0::2] | (c[..., 1::2] << 4)
    return np.ascontiguousarray(words), np.ascontiguousarray(byte.astype(np.uint8).reshape(k // 512, 16, n))


def unpack_weight(words, scales, fmt):
    g, p, n, _ = words.shape
    if fmt == "e4m3":
        vals = np.ascontiguousarray(words).view(ml_dtypes.float8_e4m3fn).astype(np.float64)
    else:
        nib = np.empty((g, p, n, 4), np.uint8)
        nib[..., 0::2] = words & 0xF
        nib[..., 1::2] = words >> 4
        vals = E2M1[nib]
    vals = vals * np.repeat(np.exp2(scales.astype(np.float64) - 127.0), 8, axis=1)[..., None]
    return vals.transpose(0, 1, 3, 2).reshape(g * 512, n)
def pack4(w):
    words, scales = pack_weight(w, "e2m1")
    return words.reshape(words.shape[0], 128, -1), scales


def unpack4(words, scales):
    return unpack_weight(words.reshape(words.shape[0], 128, -1, 2), scales, "e2m1")


T, A, B = 1536, 1024, 1024

SUM_GAIN, DIFF_GAIN = 0.8, 0.3


def draw0():
    s = mx_kscale(A)
    u = mx_kscale(T)
    wd = DIFF_GAIN * np.random.standard_normal((A, B)) / np.sqrt(A) / s[:, None]
    wd_words, wd_scales = pack4(wd)
    return {"x": bf(np.random.standard_normal((T, A)) * s * u[:, None]),
            "ws": bf(SUM_GAIN * np.random.standard_normal((A, B)) / np.sqrt(A) / s[:, None]),
            "wd_words": wd_words,
            "wd_scales": wd_scales,
            "noise": bf((1.0 + 0.5 * np.random.random(T)) * u ** 2)}


def core(x, ws, wd_words, wd_scales, noise):
    xq = mxq(f64(x), 1, "e4m3")
    total = xq @ mxq(f64(ws), 0, "e4m3")
    diff = xq @ unpack4(wd_words, wd_scales)
    r = diff / (total ** 2 + f64(noise)[:, None])
    return mxq(r, 0, "e4m3").T @ mxq(total, 0, "e4m3")


def e4m3fn_bytes(y):
    return np.clip(np.asarray(y, np.float64), -448.0, 448.0).astype(np.float32).astype(ml_dtypes.float8_e4m3fn).view(np.uint8)


def e4m3fn_values(b):
    return np.asarray(b, np.uint8).view(ml_dtypes.float8_e4m3fn).astype(np.float64)


def setup_inputs():
    d = draw0()
    x0 = np.asarray(d['ws']).astype(np.float64)
    s = (np.max(np.abs(x0), axis=(1,), keepdims=True) / 448.0).astype(np.float32)
    out = {}
    for k, v in d.items():
        if k == 'ws':
            out['ws_bytes'] = e4m3fn_bytes(x0 / s.astype(np.float64))
            out['ws_scale'] = s
        else:
            out[k] = v
    return out


def reference(x, ws_bytes, ws_scale, wd_words, wd_scales, noise):
    return core(x, e4m3fn_values(ws_bytes) * ws_scale.astype(np.float64), wd_words, wd_scales, noise)

from contextlib import ExitStack

import concourse.mybir as mybir
from concourse.masks import make_identity

M, K, B = 1536, 1024, 1024
FLOPS = 3 * 2 * M * K * B

F32 = mybir.dt.float32
BF16 = mybir.dt.bfloat16
I32 = mybir.dt.int32
U32 = mybir.dt.uint32
U8 = mybir.dt.uint8
FP8 = mybir.dt.float8_e4m3fn
FP8X4 = mybir.dt.float8_e4m3fn_x4
FP4X4 = mybir.dt.float4_e2m1fn_x4
ACT = mybir.ActivationFunctionType
MULT = mybir.AluOpType.mult

P = 128
PACK = 4
PASS = P * PACK
KG = K // PASS
MG = M // PASS
CB = 256
NCB = B // CB
UNITS = MG * NCB
HALVES = CB // P
WIDEN_V = 0
REC_G = 2
LAG = 2


def tile_monopulse_ratio_matrix_s11_kernel(tc, x, ws_bytes, ws_scale, wd_words, wd_scales, noise, out):
    nc = tc.nc
    with ExitStack() as ctx:
        keep = ctx.enter_context(tc.tile_pool(name="keep", bufs=1))
        work = ctx.enter_context(tc.tile_pool(name="work", bufs=2))
        psum = ctx.enter_context(tc.psum_pool(name="psum", bufs=2))

        x_raw = [keep.tile([P, PACK, K], BF16, name="x_raw%d" % g) for g in range(MG)]
        x_codes = [keep.tile([P, KG, PASS], U32, name="x_codes%d" % g, align_bytes=64) for g in range(MG)]
        x_planes = [keep.tile([P, KG, PASS], U8, name="x_planes%d" % g, align_bytes=64) for g in range(MG)]
        ws_raw = [keep.tile([P, PACK, B], U8, name="ws_raw%d" % g, align_bytes=64) for g in range(KG)]
        ws_factor = keep.tile([P, KG, PACK], F32, name="ws_factor")
        ws_codes = [keep.tile([P, KG, CB], U32, name="ws_codes%d" % j, align_bytes=64) for j in range(NCB)]
        ws_planes = [keep.tile([P, KG, CB], U8, name="ws_planes%d" % j, align_bytes=64) for j in range(NCB)]
        wd_codes = keep.tile([P, KG, 2 * B], U8, name="wd_codes", align_bytes=64)
        wd_planes = keep.tile([P, KG, B], U8, name="wd_planes", align_bytes=64)
        noise_raw = keep.tile([P, MG, PACK], BF16, name="noise_raw")
        noise_col = keep.tile([P, MG, PACK], F32, name="noise_col")
        s_codes = [keep.tile([P, B], U32, name="s_codes%d" % g, align_bytes=64) for g in range(MG)]
        s_planes = [keep.tile([P, B], U8, name="s_planes%d" % g, align_bytes=64) for g in range(MG)]
        r_codes = [keep.tile([P, B], U32, name="r_codes%d" % g, align_bytes=64) for g in range(MG)]
        r_planes = [keep.tile([P, B], U8, name="r_planes%d" % g, align_bytes=64) for g in range(MG)]
        ident = keep.tile([P, P], F32, name="ident")
        one = keep.tile([P, 1], F32, name="one")

        nc.scalar.dma_start(out=ws_factor[:], in_=ws_scale.rearrange("(g p t) o -> p g (t o)", p=P, t=PACK))
        nc.scalar.dma_start(out=noise_raw[:], in_=noise.rearrange("(g p t) -> p g t", p=P, t=PACK))
        ws_rows = ws_bytes.rearrange("(g p t) n -> g p t n", p=P, t=PACK)
        x_rows = x.rearrange("(g p t) k -> g p t k", p=P, t=PACK)
        nc.vector.memset(wd_planes[:].rearrange("p g n -> p (g n)").bitcast(I32), 0)
        nc.vector.memset(one[:], 1.0)
        nc.sync.dma_start(out=ws_raw[0][:], in_=ws_rows[0])
        for t in (0, 1):
            nc.sync.dma_start(out=x_raw[0][:, t, :], in_=x_rows[0][:, t, :])
        nc.sync.dma_start(out=ws_raw[1][:], in_=ws_rows[1])
        for t in (2, 3):
            nc.sync.dma_start(out=x_raw[0][:, t, :], in_=x_rows[0][:, t, :])
        nc.sync.dma_start(out=x_raw[1][:], in_=x_rows[1])
        nc.sync.dma_start(out=x_raw[2][:], in_=x_rows[2])
        nc.sync.dma_start(out=wd_codes[:], in_=wd_words.rearrange("g p n -> p g n"))
        for q in range(4):
            nc.sync.dma_start(
                out=wd_planes[32 * q : 32 * q + 4, :, :].bitcast(I32),
                in_=wd_scales[:, 4 * q : 4 * q + 4, :].rearrange("g r n -> r g n").bitcast(I32),
            )
        make_identity(nc, ident[:])
        warm = work.tile([P, 1], F32, name="warm")
        nc.scalar.activation(out=warm[:], in_=one[:], func=ACT.Abs_reciprocal_sqrt)

        live = {}

        def ws_widen(j, g):
            if g == 0:
                live["wide", j] = work.tile([P, KG, PACK, CB], BF16, name="wide", tag="wide", bufs=2, align_bytes=64)
            for t in range(PACK):
                dst = live["wide", j][:, g, t, :]
                src = ws_raw[g][:, t, j * CB : (j + 1) * CB].bitcast(FP8)
                if t < WIDEN_V:
                    nc.vector.tensor_scalar(out=dst, in0=src, scalar1=ws_factor[:, g, t : t + 1], scalar2=None, op0=MULT)
                else:
                    nc.scalar.activation(out=dst, in_=src, func=ACT.Copy, scale=ws_factor[:, g, t : t + 1])

        def ws_interleave(j, g):
            if ("wsg", j) not in live:
                live["wsg", j] = work.tile([P, KG, CB, PACK], BF16, name="ws_grouped", tag="ws_grouped", bufs=2, align_bytes=64)
            nc.vector.tensor_copy(out=live["wsg", j][:, g, :, :], in_=live["wide", j][:, g, :, :].rearrange("p t n -> p n t"))

        def ws_quantise(j, lo, hi):
            nc.vector.quantize_mx(
                out=ws_codes[j][:, lo:hi, :].rearrange("p g n -> p (g n)").bitcast(FP8X4),
                scales=ws_planes[j][:, lo:hi, :].rearrange("p g n -> p (g n)"),
                in_=live["wsg", j][:, lo:hi, :, :].rearrange("p g n t -> p (g n t)"),
            )

        def x_transpose(gm, t):
            bank = psum.tile([P, KG, 2, P], F32, name="xt", tag=("o", "d")[t % 2], bufs=2)
            words = x_raw[gm][:].bitcast(F32)
            for g in range(KG):
                for u in range(2):
                    nc.tensor.transpose(bank[:, g, u, :], words[:, t, 2 * P * g + u : 2 * P * (g + 1) : 2], ident[:])
            live["xt", gm, t] = bank

        def x_copy(gm, t):
            if ("xg", gm) not in live:
                live["xg", gm] = work.tile([P, KG, PASS, PACK], BF16, name="x_grouped", tag="x_grouped", bufs=2, align_bytes=64)
            dst = live["xg", gm][:].bitcast(F32)[:, :, t * P : (t + 1) * P, :]
            src = live.pop(("xt", gm, t))[:].rearrange("p g u r -> p g r u")
            if t % 2:
                nc.scalar.copy(out=dst, in_=src)
            else:
                nc.vector.tensor_copy(out=dst, in_=src)

        def x_quantise_all(gm):
            nc.vector.quantize_mx(
                out=x_codes[gm][:].rearrange("p g r -> p (g r)").bitcast(FP8X4), scales=x_planes[gm][:].rearrange("p g r -> p (g r)"),
                in_=live["xg", gm][:].rearrange("p g r t -> p (g r t)"),
            )

        def x_quantise(gm, g, lo, hi):
            cols = slice(lo * P, hi * P)
            nc.vector.quantize_mx(
                out=x_codes[gm][:, g, cols].bitcast(FP8X4), scales=x_planes[gm][:, g, cols],
                in_=live["xg", gm][:, g, cols, :].rearrange("p r t -> p (r t)"),
            )

        def project(u, h, tag, bufs, codes, planes, first, words_per_col, dtype):
            gm = u % MG
            bank = psum.tile([P, PACK, P], F32, name="bank_" + tag, tag=tag, bufs=bufs)
            c0 = first + h * P
            for t in range(PACK):
                rows = slice(t * P, (t + 1) * P)
                for g in range(KG):
                    nc.tensor.matmul_mx(
                        out=bank[:, t, :],
                        lhsT=x_codes[gm][:, g, rows].bitcast(FP8X4), lhsT_scale=x_planes[gm][:, g, rows],
                        rhs=codes[:, g, words_per_col * c0 : words_per_col * (c0 + P)].bitcast(dtype), rhs_scale=planes[:, g, c0 : c0 + P],
                        start=(g == 0), stop=(g == KG - 1),
                    )
            live[tag, u, h] = bank

        def project_s(u):
            for h in range(HALVES):
                project(u, h, "s", 4, ws_codes[u // MG], ws_planes[u // MG], 0, 1, FP8X4)

        def project_d(u):
            for h in range(HALVES):
                project(u, h, "d", 2, wd_codes, wd_planes, u // MG * CB, 2, FP4X4)

        def s_round(u, h):
            if h == 0:
                live["s16", u] = work.tile([P, CB, PACK], BF16, name="s16", tag="s16", bufs=3, align_bytes=64)
            nc.vector.tensor_copy(out=live["s16", u][:, h * P : (h + 1) * P, :], in_=live["s", u, h][:].rearrange("p t b -> p b t"))

        def s_square(u, h):
            if ("sq", u) not in live:
                live["sq", u] = work.tile([P, PACK, CB], F32, name="square", tag="square", bufs=2)
            nc.scalar.activation(out=live["sq", u][:, :, h * P : (h + 1) * P], in_=live["s", u, h][:], func=ACT.Square)

        def root(u):
            gm = u % MG
            rs = work.tile([P, PACK, CB], F32, name="root", tag="root", bufs=2)
            for t in range(PACK):
                nc.scalar.activation(out=rs[:, t, :], in_=live["sq", u][:, t, :], func=ACT.Abs_reciprocal_sqrt, bias=noise_col[:, gm, t : t + 1])
            live["rs", u] = rs

        def reciprocal(u):
            rec = work.tile([P, CB, PACK], F32, name="rec", tag="rec", bufs=3)
            for h in range(HALVES):
                src = live["rs", u][:, :, h * P : (h + 1) * P].rearrange("p t b -> p b t")
                dst = rec[:, h * P : (h + 1) * P, :]
                if h < REC_G:
                    nc.gpsimd.tensor_tensor(out=dst, in0=src, in1=src, op=MULT)
                else:
                    nc.scalar.activation(out=dst, in_=src, func=ACT.Square)
            live["rec", u] = rec

        def ratio(u, h):
            if h == 0:
                live["r16", u] = work.tile([P, CB, PACK], BF16, name="r16", tag="r16", bufs=3, align_bytes=64)
            nc.vector.tensor_tensor(
                out=live["r16", u][:, h * P : (h + 1) * P, :], in0=live["d", u, h][:].rearrange("p t b -> p b t"),
                in1=live["rec", u][:, h * P : (h + 1) * P, :], op=MULT,
            )

        def quantise(kind, u, codes, planes):
            j, gm = divmod(u, MG)
            cols = slice(j * CB, (j + 1) * CB)
            nc.vector.quantize_mx(
                out=codes[gm][:, cols].bitcast(FP8X4), scales=planes[gm][:, cols],
                in_=live.pop((kind, u))[:].rearrange("p b t -> p (b t)"),
            )

        def out_pass(bank, part, row, c0, width, gm):
            nc.tensor.matmul_mx(
                out=bank[:, part : part + width],
                lhsT=r_codes[gm][:, row * P : (row + 1) * P].bitcast(FP8X4), lhsT_scale=r_planes[gm][:, row * P : (row + 1) * P],
                rhs=s_codes[gm][:, c0 : c0 + width].bitcast(FP8X4), rhs_scale=s_planes[gm][:, c0 : c0 + width],
                start=(gm == 0), stop=(gm == MG - 1),
            )

        def out_wide(row, half):
            bank = psum.tile([P, 512], F32, name="ob", tag="o", bufs=2)
            for gm in range(MG):
                out_pass(bank, 0, row, half * 512, 512, gm)
            return bank, out[row * P : (row + 1) * P, half * 512 : (half + 1) * 512], 1

        def out_pair(pair, j):
            bank = psum.tile([P, 512], F32, name="ob", tag="o", bufs=2)
            for i in range(2):
                for gm in range(MG):
                    out_pass(bank, i * CB, 2 * pair + i, j * CB, CB, gm)
            return bank, out[pair * CB : (pair + 1) * CB, j * CB : (j + 1) * CB].rearrange("(i p) c -> p i c", p=P), 2

        def drain(item, on_vector):
            bank, dst, rows = item
            res = work.tile([P, 512], F32, name="res", tag="res", bufs=4)
            if on_vector:
                nc.vector.tensor_copy(out=res[:], in_=bank[:])
            else:
                nc.scalar.copy(out=res[:], in_=bank[:])
            src = res[:] if rows == 1 else res[:].rearrange("p (i c) -> p i c", i=2)
            nc.sync.dma_start(out=dst, in_=src)

        OUT = {
            5: [(out_pair, 0, 0)],
            6: [],
            7: [(out_pair, 0, 1)],
            8: [(out_wide, 2, 0)],
            9: [(out_wide, 3, 0)],
            10: [(out_pair, 0, 2), (out_pair, 1, 2)],
            11: [(out_wide, 4, 0), (out_wide, 5, 0)],
            12: [(out_pair, 0, 3), (out_pair, 1, 3)],
            13: [(out_wide, 4, 1), (out_wide, 5, 1)],
        }

        WS_STEPS = {
            0: [(ws_widen, (1, 1))],
            1: [(ws_interleave, (1, 0)), (ws_interleave, (1, 1)), (ws_widen, (2, 0))],
            2: [(ws_quantise, (1, 0, KG)), (ws_widen, (2, 1))],
            3: [(ws_interleave, (2, 0)), (ws_interleave, (2, 1))],
            4: [(ws_quantise, (2, 0, KG)), (ws_widen, (3, 0))],
            5: [(ws_widen, (3, 1))],
            6: [(ws_interleave, (3, 0)), (ws_interleave, (3, 1))],
            7: [(ws_quantise, (3, 0, KG))],
        }

        nc.vector.tensor_copy(out=noise_col[:], in_=noise_raw[:])
        for t in range(PACK):
            x_transpose(0, t)
        ws_widen(0, 0)
        x_copy(0, 0)
        ws_interleave(0, 0)
        x_copy(0, 1)
        ws_widen(0, 1)
        ws_quantise(0, 0, 1)
        for g in range(KG):
            x_quantise(0, g, 0, 2)
        x_copy(0, 2)
        x_copy(0, 3)
        ws_interleave(0, 1)
        for g in range(KG):
            x_quantise(0, g, 2, 4)
        ws_quantise(0, 1, 2)
        for t in range(PACK):
            x_transpose(1, t)
        project_s(0)
        for t in range(PACK):
            x_copy(1, t)
        ws_widen(1, 0)

        last = [(row, half) for row in (6, 7) for half in range(2)]
        tail = []
        for k in range(UNITS + LAG):
            if k == 0:
                for t in range(PACK):
                    x_transpose(2, t)
            if k >= LAG:
                project_d(k - LAG)
            items = [f(a, b) for f, a, b in OUT.get(k, [])]
            if k >= UNITS:
                if k == UNITS:
                    tail = [psum.tile([P, 512], F32, name="tb", tag="s", bufs=4) for i in range(4)]
                for bank, (row, half) in zip(tail, last):
                    out_pass(bank, 0, row, half * 512, 512, k - UNITS)
            if k == 0:
                x_quantise_all(1)
            if k < UNITS:
                for h in range(HALVES):
                    s_round(k, h)
                for h in range(HALVES):
                    s_square(k, h)
            if k == 0:
                for t in range(PACK):
                    x_copy(2, t)
            if k < UNITS:
                root(k)
                reciprocal(k)
            if k >= LAG:
                ratio(k - LAG, 0)
            if k < UNITS:
                quantise("s16", k, s_codes, s_planes)
            if k == 0:
                x_quantise_all(2)
            if k >= LAG:
                ratio(k - LAG, 1)
            for f, args in WS_STEPS.get(k, []):
                f(*args)
            if k + 1 < UNITS:
                project_s(k + 1)
            for i, item in enumerate(items):
                drain(item, k >= UNITS and i % 2 == 0)
            if k >= LAG:
                quantise("r16", k - LAG, r_codes, r_planes)
        for bank, (row, half) in zip(tail, last):
            out_pass(bank, 0, row, half * 512, 512, MG - 1)
        for i, (bank, (row, half)) in enumerate(zip(tail, last)):
            drain((bank, out[row * P : (row + 1) * P, half * 512 : (half + 1) * 512], 1), i % 2 == 0)
